import numpy as np
import ml_dtypes


def mxq(x, axis, fmt="e4m3"):
    dtype, down = {"e4m3": (ml_dtypes.float8_e4m3fn, 7), "e5m2": (ml_dtypes.float8_e5m2, 14)}[fmt]
    v = np.moveaxis(np.asarray(x, np.float32).astype(ml_dtypes.bfloat16).astype(np.float64), axis, -1)
    blocks = v.reshape(v.shape[:-1] + (-1, 32))
    amax = np.abs(blocks).max(-1, keepdims=True)
    byte = np.maximum(np.where(amax > 0, np.frexp(amax)[1] - 1 + 127, 0) - down, 1)
    scale = np.exp2(byte - 127.0)
    codes = (blocks / scale).astype(np.float32).astype(dtype).astype(np.float64)
    return np.moveaxis((codes * scale).reshape(v.shape), -1, axis)


WIDE = False


def mx_kscale(k):
    if not WIDE:
        return np.ones(k)
    levels = np.array([10, -10, 5, -5, 0])
    if k % 512:
        return np.exp2(np.random.permutation(np.resize(levels, k // 32))).repeat(32)
    a = np.empty((k // 512, 16))
    for p in range(k // 512):
        a[p, :8] = np.random.permutation(np.resize(levels, 8))
        for g in range(8):
            far = levels[np.abs(levels - a[p, g]) >= 10]
            a[p, g + 8] = far[np.random.randint(len(far))]
    return np.exp2(a.ravel()).repeat(32)


def f64(x):
    return np.asarray(x).astype(np.float64)


def striped8(idx):
    return np.asarray(idx).reshape(8, -1, 16).transpose(0, 2, 1).reshape(128, -1).astype(np.uint16)


def unstriped8(offs):
    return offs.reshape(8, 16, -1).transpose(0, 2, 1).reshape(8, -1).astype(np.int64)


def pick8(x, idx, run):
    r = np.arange(len(x))
    return x[r[:, None], idx[r % (8 * run) // run]]


E2M1 = np.array([0.0, 0.5, 1.0, 1.5, 2.0, 3.0, 4.0, 6.0, -0.0, -0.5, -1.0, -1.5, -2.0, -3.0, -4.0, -6.0])


def pack_weight(w, fmt):
    k, n = w.shape
    w = f64(np.asarray(w, np.float32).astype(ml_dtypes.bfloat16)).reshape(k // 32, 32, n)
    amax = np.abs(w).max(1)
    if fmt == "e4m3":
        byte = np.frexp(amax)[1] - 1 + 127 - 7
    else:
        mant, ex = np.frexp(amax / 6.0)
        byte = np.where(mant > 0.5, ex, ex - 1) + 127
    byte = np.clip(np.where(amax > 0, byte, 1), 1, 254)
    scaled = (w * np.exp2(127.0 - byte)[:, None, :]).reshape(k, n).astype(np.float32)
    by_word = np.ascontiguousarray(scaled.reshape(k // 512, 128, 4, n).transpose(0, 1, 3, 2))
    if fmt == "e4m3":
        words = by_word.astype(ml_dtypes.float8_e4m3fn).view(np.uint8)
    else:
        c = by_word.astype(ml_dtypes.float4_e2m1fn).view(np.uint8) & 0xF
        words = (c[..., 0::2] | (c[..., 1::2] << 4)).reshape(k // 512, 128, 2 * n)
    return np.ascontiguousarray(words), np.ascontiguousarray(byte.astype(np.uint8).reshape(k // 512, 16, n))


def unpack_weight(words, scales, fmt):
    g, _, n = scales.shape
    words = np.ascontiguousarray(words).reshape(g, 128, n, -1)
    if fmt == "e4m3":
        vals = words.view(ml_dtypes.float8_e4m3fn).astype(np.float64)
    else:
        nib = np.empty((g, 128, n, 4), np.uint8)
        nib[..., 0::2] = words & 0xF
        nib[..., 1::2] = words >> 4
        vals = E2M1[nib]
    vals = vals * np.repeat(np.exp2(scales.astype(np.float64) - 127.0), 8, axis=1)[..., None]
    return vals.transpose(0, 1, 3, 2).reshape(g * 512, n)


D, V, Q, I = 512, 2048, 128, 512


def setup_inputs():
    n = np.random.standard_normal
    idx = np.stack([np.random.permutation(V)[:I] for _ in range(8)])
    fd = mx_kscale(D)
    vocp = pack_weight(n((D, V)) / fd[:, None], "e4m3")
    return {
        "hid": (n((D, Q)) * 0.7 / np.sqrt(D) * fd[:, None]).astype(np.float32),
        "voc_words": vocp[0],
        "voc_scales": vocp[1],
        "lpo": (np.random.uniform(-8.2, -7.2, (Q, I))).astype(np.float32),
        "adv": (1.0 * n((Q, I))).astype(np.float32),
        "dhid": (n((D, Q)) * 1.0 / np.sqrt(D) * fd[:, None]).astype(np.float32),
        "base": (0.5 * n((Q, V))).astype(np.float32),
        "offs": striped8(idx),
    }


def reference(hid, voc_words, voc_scales, lpo, adv, dhid, base, offs):
    idx = unstriped8(offs)
    vocu = unpack_weight(voc_words, voc_scales, "e4m3")
    hidq = mxq(f64(hid), 0, "e4m3")
    a = hidq.T @ vocu
    dhidq = mxq(f64(dhid), 0, "e4m3")
    ta = dhidq.T @ vocu
    p = np.exp(a)
    z = np.sum(p, axis=1, keepdims=True)
    r = np.exp(pick8(a, idx, 16) - np.log(z) - f64(lpo))
    dz = np.sum(f64(adv) * r * (-1.0), axis=1, keepdims=True) / z
    xp = ta * p
    xz = np.sum(xp, axis=1, keepdims=True)
    xr = (pick8(ta, idx, 16) - xz / z) * r
    xdz = (np.sum(xr * f64(adv) * (-1.0), axis=1, keepdims=True) - xz * np.sum(f64(adv) * r * (-1.0), axis=1, keepdims=True) / z) / z
    xe1 = xr * f64(adv)
    xs1 = np.zeros((Q, V))
    xs1[np.arange(Q)[:, None], idx[np.arange(Q) % 128 // 16]] = xe1
    xda = xdz * p + xp * dz + xs1
    y = xda + f64(base)
    return y

@@ -1,0 +1,203 @@
+from contextlib import ExitStack
+
+import concourse.mybir as mybir
+from concourse.masks import make_identity
+
+F32 = mybir.dt.float32
+BF16 = mybir.dt.bfloat16
+I32 = mybir.dt.int32
+U32 = mybir.dt.uint32
+U16 = mybir.dt.uint16
+U8 = mybir.dt.uint8
+FP8X4 = mybir.dt.float8_e4m3fn_x4
+ALU = mybir.AluOpType
+ACT = mybir.ActivationFunctionType
+AX = mybir.AxisListType
+
+P = 128
+D, V, Q, NL = 512, 2048, 128, 512
+PACK = 4
+CH = 512
+NCH = V // CH
+FLOPS = 2 * 2 * D * V * Q
+
+
+def tile_attend_hvpolicyratio_heads_kernel(tc, hid, voc_words, voc_scales, lpo, adv, dhid, base, offs, out):
+    nc = tc.nc
+    with ExitStack() as ctx:
+        sb = ctx.enter_context(tc.tile_pool(name="sb", bufs=1))
+        ps = ctx.enter_context(tc.psum_pool(name="ps", bufs=1))
+
+        def tile(name, width, dtype=F32):
+            return sb.tile([P, width], dtype, name=name, align_bytes=64)
+
+        def chunk(c):
+            return slice(c * CH, (c + 1) * CH)
+
+        voc_plane = tile("voc_plane", CH, U8)
+        nc.gpsimd.memset(voc_plane[:].bitcast(I32), 0)
+        def load_scales(queue, g):
+            queue.dma_start(
+                out=voc_plane[32 * g : 32 * g + 16, :].bitcast(I32),
+                in_=voc_scales[0, 4 * g : 4 * g + 4, :].bitcast(I32).rearrange("j (c w) -> c j w", c=NCH),
+            )
+
+        for g in [2,3]:
+            load_scales(nc.scalar, g)
+        words = voc_words[0].rearrange("p n t -> p (n t)").bitcast(I32)
+        raw, voc = {}, {}
+        for name in ["hid","dhid","voc0","voc1","voc2","voc3"]:
+            if name.startswith("voc"):
+                c = int(name[3:])
+                voc[c] = tile(name, CH, U32)
+                nc.sync.dma_start(out=voc[c][:].bitcast(I32), in_=words[:, chunk(c)])
+            else:
+                raw[name] = tile(name + "_raw", PACK * Q)
+                nc.sync.dma_start(out=raw[name][:], in_={"hid": hid, "dhid": dhid}[name].rearrange("(p j) q -> p (j q)", j=PACK))
+            if name == "hid":
+                for g in [0,1]:
+                    load_scales(nc.sync, g)
+        offsets = sb.tile([P, NL // 16], U16, name="offsets")
+        nc.sync.dma_start(offsets[:], offs)
+        lpo_sb = tile("lpo_sb", NL)
+        nc.sync.dma_start(out=lpo_sb[:], in_=lpo)
+        adv_sb = tile("adv_sb", NL)
+        nc.sync.dma_start(out=adv_sb[:], in_=adv)
+        base_sb = tile("base_sb", V)
+        for h in range(2):
+            nc.sync.dma_start(out=base_sb[:, h * 1024 : (h + 1) * 1024], in_=base[:, h * 1024 : (h + 1) * 1024])
+
+        warm = tile("warm", 1)
+        nc.gpsimd.memset(warm[:], 0.0)
+        warm_out = tile("warm_out", 1)
+        nc.scalar.activation(warm_out[:], warm[:], ACT.Exp)
+
+        ident = tile("ident", P)
+        make_identity(nc, ident[:])
+        xs1 = tile("xs1", V)
+        nc.gpsimd.memset(xs1[:], 0.0)
+
+        codes, planes, grouped = {}, {}, {}
+        for name in ("hid", "dhid"):
+            grouped[name] = tile(name + "_grouped", PACK * Q, BF16)
+            dst = grouped[name][:].rearrange("p (c i t) -> p c t i", i=4, t=PACK)
+            src = raw[name][:].rearrange("p (t c i) -> p c t i", i=4, t=PACK)
+            if name == "hid":
+                nc.vector.tensor_copy(out=dst, in_=src)
+            else:
+                nc.vector.tensor_copy(out=dst, in_=src)
+        for name in ("hid", "dhid"):
+            codes[name] = tile(name + "_codes", Q, U32)
+            planes[name] = tile(name + "_plane", Q, U8)
+            nc.vector.quantize_mx(out=codes[name][:].bitcast(FP8X4), scales=planes[name][:], in_=grouped[name][:])
+
+        a_sb = tile("a_sb", V)
+        ta_sb = tile("ta_sb", V)
+        tops = tile("tops", NCH)
+        ta_bank = {}
+        for step in ["a0","t0","a1","t1","a2","t2","a3","t3"]:
+            name, c = {"a": "hid", "t": "dhid"}[step[0]], int(step[1])
+            bank = ps.tile([P, CH], F32, name="%s_bank%d" % (name, c), tag="%s_bank%d" % (name, c))
+            nc.tensor.matmul_mx(
+                out=bank[:], lhsT=codes[name][:].bitcast(FP8X4), lhsT_scale=planes[name][:],
+                rhs=voc[c][:].bitcast(FP8X4), rhs_scale=voc_plane[4 * c :, :], start=True, stop=True,
+            )
+            if name == "hid":
+                nc.vector.tensor_scalar(a_sb[:, chunk(c)], bank[:], 1.0, None, ALU.mult, ALU.max, accum_out=tops[:, c : c + 1])
+            else:
+                ta_bank[c] = bank
+                if c in [0,1,2,3]:
+                    nc.scalar.copy(out=ta_sb[:, chunk(c)], in_=bank[:])
+        neg_top = tile("neg_top", 1)
+        nc.vector.tensor_reduce(neg_top[:], tops[:], AX.X, ALU.max, negate=True)
+
+        gap = tile("gap", NL)
+        nc.vector.tensor_tensor(gap[:], a_sb[:].indirect(offsets[:]), lpo_sb[:], ALU.subtract)
+
+        p = tile("p", V)
+        NX = 2
+        parts = [slice(h * V // NX, (h + 1) * V // NX) for h in range(NX)]
+        z_parts = tile("z_parts", NX)
+        for h, cols in enumerate(parts):
+            nc.scalar.activation(p[:, cols], a_sb[:, cols], ACT.Exp, bias=neg_top[:], accum_out=z_parts[:, h : h + 1])
+        z = tile("z", 1)
+        z_copy = tile("z_copy", NX)
+        nc.scalar.activation(z_copy[:], z_parts[:], ACT.Copy, accum_out=z[:])
+        e = tile("e", NL)
+        nc.scalar.activation(e[:], gap[:], ACT.Exp, bias=neg_top[:])
+        rz = tile("rz", 1)
+
+        MODES = [2,1,1,1]
+        ar = tile("ar", NL)
+        s1 = tile("s1", 1)
+        ndz = tile("ndz", 1)
+        nrz = tile("nrz", 1)
+        nxp = tile("nxp", V)
+        nxz = tile("nxz", NX)
+        y1 = tile("y1", V)
+        y2 = tile("y2", V)
+        turned = tile("turned", V)
+        sums, back = {}, {}
+
+        def turn_into(c, src, first, last):
+            for j in range(CH // P):
+                nc.tensor.matmul(sums[c][:, j * P : (j + 1) * P], lhsT=src[:, j * P : (j + 1) * P], rhs=ident[:],
+                                 is_transpose=True, start=(first and j == 0), stop=(last and j == CH // P - 1))
+
+        def turn_back(c):
+            nc.scalar.copy(out=turned[:, chunk(c)], in_=sums[c][:])
+            back[c] = ps.tile([P, CH], F32, name="back%d" % c, tag="dhid_bank%d" % c)
+            for j in range(CH // P):
+                nc.tensor.transpose(back[c][:, j * P : (j + 1) * P], turned[:, c * CH + j * P : c * CH + (j + 1) * P], ident[:])
+
+        for c in range(NCH):
+            sums[c] = ps.tile([P, CH], F32, name="sum%d" % c, tag="hid_bank%d" % c)
+            turn_into(c, base_sb[:, chunk(c)], True, False)
+        for h, cols in enumerate(parts):
+            nc.vector.scalar_tensor_tensor(nxp[:, cols], ta_sb[:, cols], -1.0, p[:, cols], ALU.mult, ALU.mult, accum_out=nxz[:, h : h + 1])
+        nc.vector.reciprocal(rz[:], z[:])
+        nc.vector.scalar_tensor_tensor(ar[:], e[:], rz[:], adv_sb[:], ALU.mult, ALU.mult, accum_out=s1[:])
+
+        nmu = tile("nmu", 1)
+        nmu_parts = tile("nmu_parts", NX)
+        nc.scalar.activation(nmu_parts[:], nxz[:], ACT.Copy, scale=rz[:], accum_out=nmu[:])
+        nc.scalar.activation(nrz[:], rz[:], ACT.Copy, scale=-1.0)
+        nc.scalar.activation(ndz[:], s1[:], ACT.Copy, scale=rz[:])
+        ta_l = gap
+        nc.vector.tensor_copy(ta_l[:], ta_sb[:].indirect(offsets[:]))
+        cross = tile("cross", 1)
+        nc.vector.tensor_scalar(cross[:], s1[:], nrz[:], nmu[:], ALU.mult, ALU.mult)
+        xe = tile("xe", NL)
+        s2 = tile("s2", 1)
+        nc.vector.scalar_tensor_tensor(xe[:], ta_l[:], nmu[:], ar[:], ALU.add, ALU.mult, accum_out=s2[:])
+
+        nc.vector.tensor_copy(xs1[:].indirect(offsets[:]), xe[:])
+
+        xdz = tile("xdz", 1)
+        for c in [0,1,2,3]:
+            nc.scalar.activation(y1[:, chunk(c)], nxp[:, chunk(c)], ACT.Copy, scale=ndz[:])
+            turn_into(c, y1[:, chunk(c)], False, MODES[c] == 2)
+        nc.scalar.activation(xdz[:], s2[:], ACT.Identity, scale=nrz[:], bias=cross[:])
+        for c in [0,1,2,3]:
+            if MODES[c] == 1:
+                if c in []:
+                    nc.gpsimd.tensor_scalar(y2[:, chunk(c)], p[:, chunk(c)], xdz[:], 0.0, ALU.mult, ALU.add)
+                else:
+                    nc.scalar.activation(y2[:, chunk(c)], p[:, chunk(c)], ACT.Copy, scale=xdz[:])
+                turn_into(c, y2[:, chunk(c)], False, True)
+            turn_back(c)
+
+        t2 = tile("t2", V)
+        res = tile("res", V)
+        order = [0,1,2,3]
+        for c in order:
+            listed = xs1
+            if MODES[c] == 2:
+                nc.vector.scalar_tensor_tensor(t2[:, chunk(c)], p[:, chunk(c)], xdz[:], xs1[:, chunk(c)], ALU.mult, ALU.add)
+                listed = t2
+            pieces = 2 if c == order[-1] else 1
+            for h in range(pieces):
+                lo, hi = h * CH // pieces, (h + 1) * CH // pieces
+                cols = slice(c * CH + lo, c * CH + hi)
+                nc.vector.tensor_tensor(res[:, cols], back[c][:, lo:hi], listed[:, cols], ALU.add)
+                nc.sync.dma_start(out=out[:, cols], in_=res[:, cols])

@@ -46,7 +46,7 @@ def tile_attend_hvpolicyratio_heads_kernel(tc, hid, voc_words, voc_scales, lpo, 
             load_scales(nc.scalar, g)
         words = voc_words[0].rearrange("p n t -> p (n t)").bitcast(I32)
         raw, voc = {}, {}
-        for name in ["hid","dhid","voc0","voc1","voc2","voc3"]:
+        for name in ["hid","voc1","dhid","voc2","voc3","voc0"]:
             if name.startswith("voc"):
                 c = int(name[3:])
                 voc[c] = tile(name, CH, U32)
@@ -75,11 +75,11 @@ def tile_attend_hvpolicyratio_heads_kernel(tc, hid, voc_words, voc_scales, lpo, 
         ident = tile("ident", P)
         make_identity(nc, ident[:])
         xs1 = tile("xs1", V)
-        nc.gpsimd.memset(xs1[:], 0.0)
+        nc.vector.memset(xs1[:], 0.0)
 
         codes, planes, grouped = {}, {}, {}
         for name in ("hid", "dhid"):
-            grouped[name] = tile(name + "_grouped", PACK * Q, BF16)
+            grouped[name] = sb.tile([P, PACK * Q], BF16, name=name + "_grouped", tag=name + "_grouped", align_bytes=64)
             dst = grouped[name][:].rearrange("p (c i t) -> p c t i", i=4, t=PACK)
             src = raw[name][:].rearrange("p (t c i) -> p c t i", i=4, t=PACK)
             if name == "hid":
@@ -93,21 +93,26 @@ def tile_attend_hvpolicyratio_heads_kernel(tc, hid, voc_words, voc_scales, lpo, 
 
         a_sb = tile("a_sb", V)
         ta_sb = tile("ta_sb", V)
-        tops = tile("tops", NCH)
+        tops = sb.tile([P, NCH], F32, name="tops", tag="dhid_grouped", align_bytes=64)
         ta_bank = {}
-        for step in ["a0","t0","a1","t1","a2","t2","a3","t3"]:
-            name, c = {"a": "hid", "t": "dhid"}[step[0]], int(step[1])
-            bank = ps.tile([P, CH], F32, name="%s_bank%d" % (name, c), tag="%s_bank%d" % (name, c))
+        LATE = [2,3]
+
+        def score(name, c, tag):
+            bank = ps.tile([P, CH], F32, name="%s_bank%d" % (name, c), tag=tag)
             nc.tensor.matmul_mx(
                 out=bank[:], lhsT=codes[name][:].bitcast(FP8X4), lhsT_scale=planes[name][:],
                 rhs=voc[c][:].bitcast(FP8X4), rhs_scale=voc_plane[4 * c :, :], start=True, stop=True,
             )
-            if name == "hid":
-                nc.vector.tensor_scalar(a_sb[:, chunk(c)], bank[:], 1.0, None, ALU.mult, ALU.max, accum_out=tops[:, c : c + 1])
-            else:
-                ta_bank[c] = bank
-                if c in [0,1,2,3]:
-                    nc.scalar.copy(out=ta_sb[:, chunk(c)], in_=bank[:])
+            return bank
+
+        arrival = [1, 2, 3, 0]
+        for c in arrival:
+            bank = score("hid", c, "score%d" % c)
+            nc.vector.tensor_scalar(a_sb[:, chunk(c)], bank[:], 1.0, None, ALU.mult, ALU.max, accum_out=tops[:, c : c + 1])
+        for c in [1, 0, 2, 3]:
+            ta_bank[c] = score("dhid", c, "score%d" % ((c + 1) % NCH))
+            if c not in LATE:
+                nc.scalar.copy(out=ta_sb[:, chunk(c)], in_=ta_bank[c][:])
         neg_top = tile("neg_top", 1)
         nc.vector.tensor_reduce(neg_top[:], tops[:], AX.X, ALU.max, negate=True)
 
@@ -118,7 +123,7 @@ def tile_attend_hvpolicyratio_heads_kernel(tc, hid, voc_words, voc_scales, lpo, 
         NX = 2
         parts = [slice(h * V // NX, (h + 1) * V // NX) for h in range(NX)]
         z_parts = tile("z_parts", NX)
-        for h, cols in enumerate(parts):
+        for h, cols in reversed(list(enumerate(parts))):
             nc.scalar.activation(p[:, cols], a_sb[:, cols], ACT.Exp, bias=neg_top[:], accum_out=z_parts[:, h : h + 1])
         z = tile("z", 1)
         z_copy = tile("z_copy", NX)
@@ -127,13 +132,13 @@ def tile_attend_hvpolicyratio_heads_kernel(tc, hid, voc_words, voc_scales, lpo, 
         nc.scalar.activation(e[:], gap[:], ACT.Exp, bias=neg_top[:])
         rz = tile("rz", 1)
 
-        MODES = [2,1,1,1]
+        MODES = [2,2,1,1]
         ar = tile("ar", NL)
         s1 = tile("s1", 1)
         ndz = tile("ndz", 1)
         nrz = tile("nrz", 1)
         nxp = tile("nxp", V)
-        nxz = tile("nxz", NX)
+        nxz = tile("nxz", 3)
         y1 = tile("y1", V)
         y2 = tile("y2", V)
         turned = tile("turned", V)
@@ -146,20 +151,22 @@ def tile_attend_hvpolicyratio_heads_kernel(tc, hid, voc_words, voc_scales, lpo, 
 
         def turn_back(c):
             nc.scalar.copy(out=turned[:, chunk(c)], in_=sums[c][:])
-            back[c] = ps.tile([P, CH], F32, name="back%d" % c, tag="dhid_bank%d" % c)
+            back[c] = ps.tile([P, CH], F32, name="back%d" % c, tag="score%d" % ((c + 1) % NCH))
             for j in range(CH // P):
                 nc.tensor.transpose(back[c][:, j * P : (j + 1) * P], turned[:, c * CH + j * P : c * CH + (j + 1) * P], ident[:])
 
         for c in range(NCH):
-            sums[c] = ps.tile([P, CH], F32, name="sum%d" % c, tag="hid_bank%d" % c)
+            sums[c] = ps.tile([P, CH], F32, name="sum%d" % c, tag="sum%d" % c)
             turn_into(c, base_sb[:, chunk(c)], True, False)
-        for h, cols in enumerate(parts):
-            nc.vector.scalar_tensor_tensor(nxp[:, cols], ta_sb[:, cols], -1.0, p[:, cols], ALU.mult, ALU.mult, accum_out=nxz[:, h : h + 1])
+        for n, c in enumerate(LATE):
+            nc.vector.scalar_tensor_tensor(nxp[:, chunk(c)], ta_bank[c][:], -1.0, p[:, chunk(c)], ALU.mult, ALU.mult, accum_out=nxz[:, n : n + 1])
+            nc.scalar.copy(out=ta_sb[:, chunk(c)], in_=ta_bank[c][:])
+        nc.vector.scalar_tensor_tensor(nxp[:, parts[0]], ta_sb[:, parts[0]], -1.0, p[:, parts[0]], ALU.mult, ALU.mult, accum_out=nxz[:, 2:3])
         nc.vector.reciprocal(rz[:], z[:])
         nc.vector.scalar_tensor_tensor(ar[:], e[:], rz[:], adv_sb[:], ALU.mult, ALU.mult, accum_out=s1[:])
 
         nmu = tile("nmu", 1)
-        nmu_parts = tile("nmu_parts", NX)
+        nmu_parts = tile("nmu_parts", 3)
         nc.scalar.activation(nmu_parts[:], nxz[:], ACT.Copy, scale=rz[:], accum_out=nmu[:])
         nc.scalar.activation(nrz[:], rz[:], ACT.Copy, scale=-1.0)
         nc.scalar.activation(ndz[:], s1[:], ACT.Copy, scale=rz[:])
@@ -191,10 +198,10 @@ def tile_attend_hvpolicyratio_heads_kernel(tc, hid, voc_words, voc_scales, lpo, 
         res = tile("res", V)
         order = [0,1,2,3]
         for c in order:
-            listed = xs1
             if MODES[c] == 2:
                 nc.vector.scalar_tensor_tensor(t2[:, chunk(c)], p[:, chunk(c)], xdz[:], xs1[:, chunk(c)], ALU.mult, ALU.add)
-                listed = t2
+        for c in order:
+            listed = t2 if MODES[c] == 2 else xs1
             pieces = 2 if c == order[-1] else 1
             for h in range(pieces):
                 lo, hi = h * CH // pieces, (h + 1) * CH // pieces

@@ -15,11 +15,21 @@ ACT = mybir.ActivationFunctionType
 AX = mybir.AxisListType
 
 P = 128
-D, V, Q, NL = 512, 2048, 128, 512
+D, V, Q, LISTED = 512, 2048, 128, 512
 PACK = 4
-CH = 512
-NCH = V // CH
+CHUNK = 512
+CHUNKS = V // CHUNK
+HALF = CHUNK // 2
+QUADRANT = 32
 FLOPS = 2 * 2 * D * V * Q
+
+ARRIVAL = (1, 2, 3, 0)
+EARLY, LATE = (1, 0), (2, 3)
+
+ON_GPSIMD = slice(0, CHUNK)
+TWO_TERMS = slice(CHUNK, CHUNK + HALF)
+THREE_TERMS = (slice(CHUNK + HALF, 2 * CHUNK), slice(2 * CHUNK, 3 * CHUNK), slice(3 * CHUNK, V))
+LAST_STORE = 128
 
 
 def tile_attend_hvpolicyratio_heads_kernel(tc, hid, voc_words, voc_scales, lpo, adv, dhid, base, offs, out):
@@ -28,49 +38,54 @@ def tile_attend_hvpolicyratio_heads_kernel(tc, hid, voc_words, voc_scales, lpo, 
         sb = ctx.enter_context(tc.tile_pool(name="sb", bufs=1))
         ps = ctx.enter_context(tc.psum_pool(name="ps", bufs=1))
 
-        def tile(name, width, dtype=F32):
-            return sb.tile([P, width], dtype, name=name, align_bytes=64)
+        def tile(name, width, dtype=F32, tag=None):
+            return sb.tile([P, width], dtype, name=name, tag=tag or name, align_bytes=64)
 
         def chunk(c):
-            return slice(c * CH, (c + 1) * CH)
+            return slice(c * CHUNK, (c + 1) * CHUNK)
 
-        voc_plane = tile("voc_plane", CH, U8)
-        nc.gpsimd.memset(voc_plane[:].bitcast(I32), 0)
+        voc_plane = tile("voc_plane", CHUNK, U8)
+        nc.vector.memset(voc_plane[:].bitcast(I32), 0)
+
         def load_scales(queue, g):
-            queue.dma_start(
-                out=voc_plane[32 * g : 32 * g + 16, :].bitcast(I32),
-                in_=voc_scales[0, 4 * g : 4 * g + 4, :].bitcast(I32).rearrange("j (c w) -> c j w", c=NCH),
-            )
+            rows = voc_scales[0, 4 * g : 4 * g + 4, :].bitcast(I32).rearrange("j (c w) -> c j w", c=CHUNKS)
+            queue.dma_start(out=voc_plane[QUADRANT * g : QUADRANT * g + 4 * CHUNKS, :].bitcast(I32), in_=rows)
 
-        for g in [2,3]:
-            load_scales(nc.scalar, g)
         words = voc_words[0].rearrange("p n t -> p (n t)").bitcast(I32)
         raw, voc = {}, {}
-        for name in ["hid","voc1","dhid","voc2","voc3","voc0"]:
-            if name.startswith("voc"):
-                c = int(name[3:])
-                voc[c] = tile(name, CH, U32)
-                nc.sync.dma_start(out=voc[c][:].bitcast(I32), in_=words[:, chunk(c)])
-            else:
-                raw[name] = tile(name + "_raw", PACK * Q)
-                nc.sync.dma_start(out=raw[name][:], in_={"hid": hid, "dhid": dhid}[name].rearrange("(p j) q -> p (j q)", j=PACK))
-            if name == "hid":
-                for g in [0,1]:
-                    load_scales(nc.sync, g)
-        offsets = sb.tile([P, NL // 16], U16, name="offsets")
+
+        def load_states(name, source):
+            raw[name] = tile(name + "_raw", PACK * Q)
+            nc.sync.dma_start(out=raw[name][:], in_=source.rearrange("(p t) q -> p (t q)", t=PACK))
+
+        def load_words(c):
+            voc[c] = tile("voc%d" % c, CHUNK, U32)
+            nc.sync.dma_start(out=voc[c][:].bitcast(I32), in_=words[:, chunk(c)])
+
+        load_scales(nc.scalar, 2)
+        load_scales(nc.scalar, 3)
+        load_states("hid", hid)
+        load_scales(nc.sync, 0)
+        load_scales(nc.sync, 1)
+        load_words(ARRIVAL[0])
+        load_states("dhid", dhid)
+        for c in ARRIVAL[1:]:
+            load_words(c)
+        offsets = sb.tile([P, LISTED // 16], U16, name="offsets")
         nc.sync.dma_start(offsets[:], offs)
-        lpo_sb = tile("lpo_sb", NL)
+        lpo_sb = tile("lpo_sb", LISTED)
         nc.sync.dma_start(out=lpo_sb[:], in_=lpo)
-        adv_sb = tile("adv_sb", NL)
+        adv_sb = tile("adv_sb", LISTED)
         nc.sync.dma_start(out=adv_sb[:], in_=adv)
         base_sb = tile("base_sb", V)
-        for h in range(2):
-            nc.sync.dma_start(out=base_sb[:, h * 1024 : (h + 1) * 1024], in_=base[:, h * 1024 : (h + 1) * 1024])
+        lower, upper = slice(0, V // 2), slice(V // 2, V)
+        for cols in (lower, upper):
+            nc.sync.dma_start(out=base_sb[:, cols], in_=base[:, cols])
 
-        warm = tile("warm", 1)
-        nc.gpsimd.memset(warm[:], 0.0)
-        warm_out = tile("warm_out", 1)
-        nc.scalar.activation(warm_out[:], warm[:], ACT.Exp)
+        zero = tile("zero", 1)
+        nc.vector.memset(zero[:], 0.0)
+        one = tile("one", 1)
+        nc.scalar.activation(one[:], zero[:], ACT.Exp)
 
         ident = tile("ident", P)
         make_identity(nc, ident[:])
@@ -79,13 +94,11 @@ def tile_attend_hvpolicyratio_heads_kernel(tc, hid, voc_words, voc_scales, lpo, 
 
         codes, planes, grouped = {}, {}, {}
         for name in ("hid", "dhid"):
-            grouped[name] = sb.tile([P, PACK * Q], BF16, name=name + "_grouped", tag=name + "_grouped", align_bytes=64)
-            dst = grouped[name][:].rearrange("p (c i t) -> p c t i", i=4, t=PACK)
-            src = raw[name][:].rearrange("p (t c i) -> p c t i", i=4, t=PACK)
-            if name == "hid":
-                nc.vector.tensor_copy(out=dst, in_=src)
-            else:
-                nc.vector.tensor_copy(out=dst, in_=src)
+            grouped[name] = tile(name + "_grouped", PACK * Q, BF16)
+            nc.vector.tensor_copy(
+                out=grouped[name][:].rearrange("p (c i t) -> p c t i", i=4, t=PACK),
+                in_=raw[name][:].rearrange("p (t c i) -> p c t i", i=4, t=PACK),
+            )
         for name in ("hid", "dhid"):
             codes[name] = tile(name + "_codes", Q, U32)
             planes[name] = tile(name + "_plane", Q, U8)
@@ -93,118 +106,143 @@ def tile_attend_hvpolicyratio_heads_kernel(tc, hid, voc_words, voc_scales, lpo, 
 
         a_sb = tile("a_sb", V)
         ta_sb = tile("ta_sb", V)
-        tops = sb.tile([P, NCH], F32, name="tops", tag="dhid_grouped", align_bytes=64)
-        ta_bank = {}
-        LATE = [2,3]
+        tops = tile("tops", CHUNKS, tag="dhid_grouped")
 
-        def score(name, c, tag):
-            bank = ps.tile([P, CH], F32, name="%s_bank%d" % (name, c), tag=tag)
+        def score(name, c, bank_number):
+            bank = ps.tile([P, CHUNK], F32, name="%s_bank%d" % (name, c), tag="score%d" % bank_number)
             nc.tensor.matmul_mx(
                 out=bank[:], lhsT=codes[name][:].bitcast(FP8X4), lhsT_scale=planes[name][:],
                 rhs=voc[c][:].bitcast(FP8X4), rhs_scale=voc_plane[4 * c :, :], start=True, stop=True,
             )
             return bank
 
-        arrival = [1, 2, 3, 0]
-        for c in arrival:
-            bank = score("hid", c, "score%d" % c)
-            nc.vector.tensor_scalar(a_sb[:, chunk(c)], bank[:], 1.0, None, ALU.mult, ALU.max, accum_out=tops[:, c : c + 1])
-        for c in [1, 0, 2, 3]:
-            ta_bank[c] = score("dhid", c, "score%d" % ((c + 1) % NCH))
-            if c not in LATE:
+        for c in ARRIVAL:
+            a_bank = score("hid", c, c)
+            nc.vector.tensor_scalar(
+                a_sb[:, chunk(c)], a_bank[:], one[:], None, ALU.mult, ALU.max, accum_out=tops[:, c : c + 1]
+            )
+        ta_bank = {}
+        for c in EARLY + LATE:
+            ta_bank[c] = score("dhid", c, (c + 1) % CHUNKS)
+            if c in EARLY:
                 nc.scalar.copy(out=ta_sb[:, chunk(c)], in_=ta_bank[c][:])
         neg_top = tile("neg_top", 1)
         nc.vector.tensor_reduce(neg_top[:], tops[:], AX.X, ALU.max, negate=True)
 
-        gap = tile("gap", NL)
+        gap = tile("gap", LISTED)
         nc.vector.tensor_tensor(gap[:], a_sb[:].indirect(offsets[:]), lpo_sb[:], ALU.subtract)
-
         p = tile("p", V)
-        NX = 2
-        parts = [slice(h * V // NX, (h + 1) * V // NX) for h in range(NX)]
-        z_parts = tile("z_parts", NX)
-        for h, cols in reversed(list(enumerate(parts))):
+        z_parts = tile("z_parts", 2)
+        for h, cols in enumerate((upper, lower)):
             nc.scalar.activation(p[:, cols], a_sb[:, cols], ACT.Exp, bias=neg_top[:], accum_out=z_parts[:, h : h + 1])
         z = tile("z", 1)
-        z_copy = tile("z_copy", NX)
+        z_copy = tile("z_copy", 2)
         nc.scalar.activation(z_copy[:], z_parts[:], ACT.Copy, accum_out=z[:])
-        e = tile("e", NL)
-        nc.scalar.activation(e[:], gap[:], ACT.Exp, bias=neg_top[:])
-        rz = tile("rz", 1)
+        r_times_z = tile("r_times_z", LISTED)
+        nc.scalar.activation(r_times_z[:], gap[:], ACT.Exp, bias=neg_top[:])
 
-        MODES = [2,2,1,1]
-        ar = tile("ar", NL)
-        s1 = tile("s1", 1)
-        ndz = tile("ndz", 1)
-        nrz = tile("nrz", 1)
-        nxp = tile("nxp", V)
-        nxz = tile("nxz", 3)
-        y1 = tile("y1", V)
-        y2 = tile("y2", V)
+        ranges = (TWO_TERMS,) + THREE_TERMS
         turned = tile("turned", V)
-        sums, back = {}, {}
+        sums, dense = {}, {}
 
-        def turn_into(c, src, first, last):
-            for j in range(CH // P):
-                nc.tensor.matmul(sums[c][:, j * P : (j + 1) * P], lhsT=src[:, j * P : (j + 1) * P], rhs=ident[:],
-                                 is_transpose=True, start=(first and j == 0), stop=(last and j == CH // P - 1))
+        def add_turned(cols, term, first=False, last=False):
+            blocks = range(cols.start, cols.stop, P)
+            for lo in blocks:
+                nc.tensor.matmul(
+                    sums[cols.start][:, lo - cols.start : lo - cols.start + P], lhsT=term[:, lo : lo + P], rhs=ident[:],
+                    is_transpose=True, start=(first and lo == blocks[0]), stop=(last and lo == blocks[-1]),
+                )
 
-        def turn_back(c):
-            nc.scalar.copy(out=turned[:, chunk(c)], in_=sums[c][:])
-            back[c] = ps.tile([P, CH], F32, name="back%d" % c, tag="score%d" % ((c + 1) % NCH))
-            for j in range(CH // P):
-                nc.tensor.transpose(back[c][:, j * P : (j + 1) * P], turned[:, c * CH + j * P : c * CH + (j + 1) * P], ident[:])
+        def turn_back(cols):
+            width, number = cols.stop - cols.start, ranges.index(cols)
+            nc.scalar.copy(out=turned[:, cols], in_=sums[cols.start][:, 0:width])
+            dense[cols.start] = ps.tile([P, CHUNK], F32, name="dense%d" % number, tag="score%d" % ((number + 1) % CHUNKS))
+            for lo in range(cols.start, cols.stop, P):
+                nc.tensor.transpose(
+                    dense[cols.start][:, lo - cols.start : lo - cols.start + P], turned[:, lo : lo + P], ident[:]
+                )
 
-        for c in range(NCH):
-            sums[c] = ps.tile([P, CH], F32, name="sum%d" % c, tag="sum%d" % c)
-            turn_into(c, base_sb[:, chunk(c)], True, False)
+        for number, cols in enumerate(ranges):
+            sums[cols.start] = ps.tile([P, CHUNK], F32, name="sum%d" % number)
+            add_turned(cols, base_sb, first=True)
+
+        neg_xp = tile("neg_xp", V)
+        neg_xz_parts = tile("neg_xz_parts", len(LATE) + 1)
         for n, c in enumerate(LATE):
-            nc.vector.scalar_tensor_tensor(nxp[:, chunk(c)], ta_bank[c][:], -1.0, p[:, chunk(c)], ALU.mult, ALU.mult, accum_out=nxz[:, n : n + 1])
+            nc.vector.scalar_tensor_tensor(
+                neg_xp[:, chunk(c)], ta_bank[c][:], -1.0, p[:, chunk(c)], ALU.mult, ALU.mult,
+                accum_out=neg_xz_parts[:, n : n + 1],
+            )
             nc.scalar.copy(out=ta_sb[:, chunk(c)], in_=ta_bank[c][:])
-        nc.vector.scalar_tensor_tensor(nxp[:, parts[0]], ta_sb[:, parts[0]], -1.0, p[:, parts[0]], ALU.mult, ALU.mult, accum_out=nxz[:, 2:3])
-        nc.vector.reciprocal(rz[:], z[:])
-        nc.vector.scalar_tensor_tensor(ar[:], e[:], rz[:], adv_sb[:], ALU.mult, ALU.mult, accum_out=s1[:])
+        inv_z = tile("inv_z", 1)
+        nc.vector.reciprocal(inv_z[:], z[:])
+        nc.vector.scalar_tensor_tensor(
+            neg_xp[:, lower], ta_sb[:, lower], -1.0, p[:, lower], ALU.mult, ALU.mult,
+            accum_out=neg_xz_parts[:, len(LATE) : len(LATE) + 1],
+        )
+        adv_r = tile("adv_r", LISTED)
+        s1 = tile("s1", 1)
+        nc.vector.scalar_tensor_tensor(adv_r[:], r_times_z[:], inv_z[:], adv_sb[:], ALU.mult, ALU.mult, accum_out=s1[:])
 
-        nmu = tile("nmu", 1)
-        nmu_parts = tile("nmu_parts", 3)
-        nc.scalar.activation(nmu_parts[:], nxz[:], ACT.Copy, scale=rz[:], accum_out=nmu[:])
-        nc.scalar.activation(nrz[:], rz[:], ACT.Copy, scale=-1.0)
-        nc.scalar.activation(ndz[:], s1[:], ACT.Copy, scale=rz[:])
-        ta_l = gap
-        nc.vector.tensor_copy(ta_l[:], ta_sb[:].indirect(offsets[:]))
+        neg_mean = tile("neg_mean", 1)
+        neg_mean_parts = tile("neg_mean_parts", len(LATE) + 1)
+        nc.scalar.activation(neg_mean_parts[:], neg_xz_parts[:], ACT.Copy, scale=inv_z[:], accum_out=neg_mean[:])
+        neg_inv_z = tile("neg_inv_z", 1)
+        nc.scalar.activation(neg_inv_z[:], inv_z[:], ACT.Copy, scale=-1.0)
+        neg_dz = tile("neg_dz", 1)
+        nc.scalar.activation(neg_dz[:], s1[:], ACT.Copy, scale=inv_z[:])
+
+        ta_listed = gap
+        nc.vector.tensor_copy(ta_listed[:], ta_sb[:].indirect(offsets[:]))
         cross = tile("cross", 1)
-        nc.vector.tensor_scalar(cross[:], s1[:], nrz[:], nmu[:], ALU.mult, ALU.mult)
-        xe = tile("xe", NL)
+        nc.vector.tensor_scalar(cross[:], s1[:], neg_inv_z[:], neg_mean[:], ALU.mult, ALU.mult)
+        base_dz_xp = tile("base_dz_xp", CHUNK)
+        halves = (slice(0, HALF), slice(HALF, CHUNK))
+
+        def add_dz_xp_to_base(cols):
+            nc.vector.scalar_tensor_tensor(
+                base_dz_xp[:, cols], neg_xp[:, cols], neg_dz[:], base_sb[:, cols], ALU.mult, ALU.add
+            )
+
+        add_dz_xp_to_base(halves[0])
+        xe1 = tile("xe1", LISTED)
         s2 = tile("s2", 1)
-        nc.vector.scalar_tensor_tensor(xe[:], ta_l[:], nmu[:], ar[:], ALU.add, ALU.mult, accum_out=s2[:])
+        nc.vector.scalar_tensor_tensor(xe1[:], ta_listed[:], neg_mean[:], adv_r[:], ALU.add, ALU.mult, accum_out=s2[:])
+        add_dz_xp_to_base(halves[1])
+        nc.vector.tensor_copy(xs1[:].indirect(offsets[:]), xe1[:])
 
-        nc.vector.tensor_copy(xs1[:].indirect(offsets[:]), xe[:])
-
+        dz_xp = tile("dz_xp", V)
+        for cols in ranges:
+            nc.scalar.activation(dz_xp[:, cols], neg_xp[:, cols], ACT.Copy, scale=neg_dz[:])
+            add_turned(cols, dz_xp, last=(cols == TWO_TERMS))
         xdz = tile("xdz", 1)
-        for c in [0,1,2,3]:
-            nc.scalar.activation(y1[:, chunk(c)], nxp[:, chunk(c)], ACT.Copy, scale=ndz[:])
-            turn_into(c, y1[:, chunk(c)], False, MODES[c] == 2)
-        nc.scalar.activation(xdz[:], s2[:], ACT.Identity, scale=nrz[:], bias=cross[:])
-        for c in [0,1,2,3]:
-            if MODES[c] == 1:
-                if c in []:
-                    nc.gpsimd.tensor_scalar(y2[:, chunk(c)], p[:, chunk(c)], xdz[:], 0.0, ALU.mult, ALU.add)
-                else:
-                    nc.scalar.activation(y2[:, chunk(c)], p[:, chunk(c)], ACT.Copy, scale=xdz[:])
-                turn_into(c, y2[:, chunk(c)], False, True)
-            turn_back(c)
+        nc.scalar.activation(xdz[:], s2[:], ACT.Identity, scale=neg_inv_z[:], bias=cross[:])
+        xdz_p = tile("xdz_p", V)
+        nc.gpsimd.tensor_scalar(xdz_p[:, ON_GPSIMD], p[:, ON_GPSIMD], xdz[:], 0.0, ALU.mult, ALU.add)
+        dense_sb = tile("dense_sb", TWO_TERMS.stop)
+        nc.gpsimd.tensor_tensor(dense_sb[:, ON_GPSIMD], xdz_p[:, ON_GPSIMD], base_dz_xp[:], ALU.add)
+        turn_back(TWO_TERMS)
+        for cols in THREE_TERMS:
+            nc.scalar.activation(xdz_p[:, cols], p[:, cols], ACT.Copy, scale=xdz[:])
+            add_turned(cols, xdz_p, last=True)
+        for cols in THREE_TERMS:
+            turn_back(cols)
+        nc.vector.scalar_tensor_tensor(
+            dense_sb[:, TWO_TERMS], p[:, TWO_TERMS], xdz[:], dense[TWO_TERMS.start][:, 0:HALF], ALU.mult, ALU.add
+        )
 
-        t2 = tile("t2", V)
-        res = tile("res", V)
-        order = [0,1,2,3]
-        for c in order:
-            if MODES[c] == 2:
-                nc.vector.scalar_tensor_tensor(t2[:, chunk(c)], p[:, chunk(c)], xdz[:], xs1[:, chunk(c)], ALU.mult, ALU.add)
-        for c in order:
-            listed = t2 if MODES[c] == 2 else xs1
-            pieces = 2 if c == order[-1] else 1
-            for h in range(pieces):
-                lo, hi = h * CH // pieces, (h + 1) * CH // pieces
-                cols = slice(c * CH + lo, c * CH + hi)
-                nc.vector.tensor_tensor(res[:, cols], back[c][:, lo:hi], listed[:, cols], ALU.add)
-                nc.sync.dma_start(out=out[:, cols], in_=res[:, cols])
+        result = tile("result", V)
+
+        def finish(engine, cols, dense_part, staged):
+            engine.tensor_tensor(staged, dense_part, xs1[:, cols], ALU.add)
+            nc.sync.dma_start(out=out[:, cols], in_=staged)
+
+        for cols in (halves[0], TWO_TERMS):
+            finish(nc.vector, cols, dense_sb[:, cols], result[:, cols])
+        for cols in THREE_TERMS[:2]:
+            finish(nc.vector, cols, dense[cols.start][:, 0 : cols.stop - cols.start], result[:, cols])
+        spent = THREE_TERMS[1].start
+        finish(nc.gpsimd, halves[1], dense_sb[:, halves[1]], turned[:, spent : spent + HALF])
+        first = THREE_TERMS[2].start
+        for cols in (slice(first, V - LAST_STORE), slice(V - LAST_STORE, V)):
+            finish(nc.vector, cols, dense[first][:, cols.start - first : cols.stop - first], result[:, cols])

from contextlib import ExitStack

import concourse.mybir as mybir
from concourse.masks import make_identity

F32 = mybir.dt.float32
BF16 = mybir.dt.bfloat16
I32 = mybir.dt.int32
U32 = mybir.dt.uint32
U16 = mybir.dt.uint16
U8 = mybir.dt.uint8
FP8X4 = mybir.dt.float8_e4m3fn_x4
ALU = mybir.AluOpType
ACT = mybir.ActivationFunctionType
AX = mybir.AxisListType

P = 128
D, V, Q, LISTED = 512, 2048, 128, 512
PACK = 4
CHUNK = 512
CHUNKS = V // CHUNK
HALF = CHUNK // 2
QUADRANT = 32
FLOPS = 2 * 2 * D * V * Q

ARRIVAL = (1, 2, 3, 0)
EARLY, LATE = (1, 0), (2, 3)

ON_GPSIMD = slice(0, CHUNK)
TWO_TERMS = slice(CHUNK, CHUNK + HALF)
THREE_TERMS = (slice(CHUNK + HALF, 2 * CHUNK), slice(2 * CHUNK, 3 * CHUNK), slice(3 * CHUNK, V))
LAST_STORE = 128


def tile_attend_hvpolicyratio_heads_kernel(tc, hid, voc_words, voc_scales, lpo, adv, dhid, base, offs, out):
    nc = tc.nc
    with ExitStack() as ctx:
        sb = ctx.enter_context(tc.tile_pool(name="sb", bufs=1))
        ps = ctx.enter_context(tc.psum_pool(name="ps", bufs=1))

        def tile(name, width, dtype=F32, tag=None):
            return sb.tile([P, width], dtype, name=name, tag=tag or name, align_bytes=64)

        def chunk(c):
            return slice(c * CHUNK, (c + 1) * CHUNK)

        voc_plane = tile("voc_plane", CHUNK, U8)
        nc.vector.memset(voc_plane[:].bitcast(I32), 0)

        def load_scales(queue, g):
            rows = voc_scales[0, 4 * g : 4 * g + 4, :].bitcast(I32).rearrange("j (c w) -> c j w", c=CHUNKS)
            queue.dma_start(out=voc_plane[QUADRANT * g : QUADRANT * g + 4 * CHUNKS, :].bitcast(I32), in_=rows)

        words = voc_words[0].rearrange("p n t -> p (n t)").bitcast(I32)
        raw, voc = {}, {}

        def load_states(name, source):
            raw[name] = tile(name + "_raw", PACK * Q)
            nc.sync.dma_start(out=raw[name][:], in_=source.rearrange("(p t) q -> p (t q)", t=PACK))

        def load_words(c):
            voc[c] = tile("voc%d" % c, CHUNK, U32)
            nc.sync.dma_start(out=voc[c][:].bitcast(I32), in_=words[:, chunk(c)])

        load_scales(nc.scalar, 2)
        load_scales(nc.scalar, 3)
        load_states("hid", hid)
        load_scales(nc.sync, 0)
        load_scales(nc.sync, 1)
        load_words(ARRIVAL[0])
        load_states("dhid", dhid)
        for c in ARRIVAL[1:]:
            load_words(c)
        offsets = sb.tile([P, LISTED // 16], U16, name="offsets")
        nc.sync.dma_start(offsets[:], offs)
        lpo_sb = tile("lpo_sb", LISTED)
        nc.sync.dma_start(out=lpo_sb[:], in_=lpo)
        adv_sb = tile("adv_sb", LISTED)
        nc.sync.dma_start(out=adv_sb[:], in_=adv)
        base_sb = tile("base_sb", V)
        lower, upper = slice(0, V // 2), slice(V // 2, V)
        for cols in (lower, upper):
            nc.sync.dma_start(out=base_sb[:, cols], in_=base[:, cols])

        zero = tile("zero", 1)
        nc.vector.memset(zero[:], 0.0)
        one = tile("one", 1)
        nc.scalar.activation(one[:], zero[:], ACT.Exp)

        ident = tile("ident", P)
        make_identity(nc, ident[:])
        xs1 = tile("xs1", V)
        nc.vector.memset(xs1[:], 0.0)

        codes, planes, grouped = {}, {}, {}
        for name in ("hid", "dhid"):
            grouped[name] = tile(name + "_grouped", PACK * Q, BF16)
            nc.vector.tensor_copy(
                out=grouped[name][:].rearrange("p (c i t) -> p c t i", i=4, t=PACK),
                in_=raw[name][:].rearrange("p (t c i) -> p c t i", i=4, t=PACK),
            )
        for name in ("hid", "dhid"):
            codes[name] = tile(name + "_codes", Q, U32)
            planes[name] = tile(name + "_plane", Q, U8)
            nc.vector.quantize_mx(out=codes[name][:].bitcast(FP8X4), scales=planes[name][:], in_=grouped[name][:])

        a_sb = tile("a_sb", V)
        ta_sb = tile("ta_sb", V)
        tops = tile("tops", CHUNKS, tag="dhid_grouped")

        def score(name, c, bank_number):
            bank = ps.tile([P, CHUNK], F32, name="%s_bank%d" % (name, c), tag="score%d" % bank_number)
            nc.tensor.matmul_mx(
                out=bank[:], lhsT=codes[name][:].bitcast(FP8X4), lhsT_scale=planes[name][:],
                rhs=voc[c][:].bitcast(FP8X4), rhs_scale=voc_plane[4 * c :, :], start=True, stop=True,
            )
            return bank

        for c in ARRIVAL:
            a_bank = score("hid", c, c)
            nc.vector.tensor_scalar(
                a_sb[:, chunk(c)], a_bank[:], one[:], None, ALU.mult, ALU.max, accum_out=tops[:, c : c + 1]
            )
        ta_bank = {}
        for c in EARLY + LATE:
            ta_bank[c] = score("dhid", c, (c + 1) % CHUNKS)
            if c in EARLY:
                nc.scalar.copy(out=ta_sb[:, chunk(c)], in_=ta_bank[c][:])
        neg_top = tile("neg_top", 1)
        nc.vector.tensor_reduce(neg_top[:], tops[:], AX.X, ALU.max, negate=True)

        gap = tile("gap", LISTED)
        nc.vector.tensor_tensor(gap[:], a_sb[:].indirect(offsets[:]), lpo_sb[:], ALU.subtract)
        p = tile("p", V)
        z_parts = tile("z_parts", 2)
        for h, cols in enumerate((upper, lower)):
            nc.scalar.activation(p[:, cols], a_sb[:, cols], ACT.Exp, bias=neg_top[:], accum_out=z_parts[:, h : h + 1])
        z = tile("z", 1)
        z_copy = tile("z_copy", 2)
        nc.scalar.activation(z_copy[:], z_parts[:], ACT.Copy, accum_out=z[:])
        r_times_z = tile("r_times_z", LISTED)
        nc.scalar.activation(r_times_z[:], gap[:], ACT.Exp, bias=neg_top[:])

        ranges = (TWO_TERMS,) + THREE_TERMS
        turned = tile("turned", V)
        sums, dense = {}, {}

        def add_turned(cols, term, first=False, last=False):
            blocks = range(cols.start, cols.stop, P)
            for lo in blocks:
                nc.tensor.matmul(
                    sums[cols.start][:, lo - cols.start : lo - cols.start + P], lhsT=term[:, lo : lo + P], rhs=ident[:],
                    is_transpose=True, start=(first and lo == blocks[0]), stop=(last and lo == blocks[-1]),
                )

        def turn_back(cols):
            width, number = cols.stop - cols.start, ranges.index(cols)
            nc.scalar.copy(out=turned[:, cols], in_=sums[cols.start][:, 0:width])
            dense[cols.start] = ps.tile([P, CHUNK], F32, name="dense%d" % number, tag="score%d" % ((number + 1) % CHUNKS))
            for lo in range(cols.start, cols.stop, P):
                nc.tensor.transpose(
                    dense[cols.start][:, lo - cols.start : lo - cols.start + P], turned[:, lo : lo + P], ident[:]
                )

        for number, cols in enumerate(ranges):
            sums[cols.start] = ps.tile([P, CHUNK], F32, name="sum%d" % number)
            add_turned(cols, base_sb, first=True)

        neg_xp = tile("neg_xp", V)
        neg_xz_parts = tile("neg_xz_parts", len(LATE) + 1)
        for n, c in enumerate(LATE):
            nc.vector.scalar_tensor_tensor(
                neg_xp[:, chunk(c)], ta_bank[c][:], -1.0, p[:, chunk(c)], ALU.mult, ALU.mult,
                accum_out=neg_xz_parts[:, n : n + 1],
            )
            nc.scalar.copy(out=ta_sb[:, chunk(c)], in_=ta_bank[c][:])
        inv_z = tile("inv_z", 1)
        nc.vector.reciprocal(inv_z[:], z[:])
        nc.vector.scalar_tensor_tensor(
            neg_xp[:, lower], ta_sb[:, lower], -1.0, p[:, lower], ALU.mult, ALU.mult,
            accum_out=neg_xz_parts[:, len(LATE) : len(LATE) + 1],
        )
        adv_r = tile("adv_r", LISTED)
        s1 = tile("s1", 1)
        nc.vector.scalar_tensor_tensor(adv_r[:], r_times_z[:], inv_z[:], adv_sb[:], ALU.mult, ALU.mult, accum_out=s1[:])

        neg_mean = tile("neg_mean", 1)
        neg_mean_parts = tile("neg_mean_parts", len(LATE) + 1)
        nc.scalar.activation(neg_mean_parts[:], neg_xz_parts[:], ACT.Copy, scale=inv_z[:], accum_out=neg_mean[:])
        neg_inv_z = tile("neg_inv_z", 1)
        nc.scalar.activation(neg_inv_z[:], inv_z[:], ACT.Copy, scale=-1.0)
        neg_dz = tile("neg_dz", 1)
        nc.scalar.activation(neg_dz[:], s1[:], ACT.Copy, scale=inv_z[:])

        ta_listed = gap
        nc.vector.tensor_copy(ta_listed[:], ta_sb[:].indirect(offsets[:]))
        cross = tile("cross", 1)
        nc.vector.tensor_scalar(cross[:], s1[:], neg_inv_z[:], neg_mean[:], ALU.mult, ALU.mult)
        base_dz_xp = tile("base_dz_xp", CHUNK)
        halves = (slice(0, HALF), slice(HALF, CHUNK))

        def add_dz_xp_to_base(cols):
            nc.vector.scalar_tensor_tensor(
                base_dz_xp[:, cols], neg_xp[:, cols], neg_dz[:], base_sb[:, cols], ALU.mult, ALU.add
            )

        add_dz_xp_to_base(halves[0])
        xe1 = tile("xe1", LISTED)
        s2 = tile("s2", 1)
        nc.vector.scalar_tensor_tensor(xe1[:], ta_listed[:], neg_mean[:], adv_r[:], ALU.add, ALU.mult, accum_out=s2[:])
        add_dz_xp_to_base(halves[1])
        nc.vector.tensor_copy(xs1[:].indirect(offsets[:]), xe1[:])

        dz_xp = tile("dz_xp", V)
        for cols in ranges:
            nc.scalar.activation(dz_xp[:, cols], neg_xp[:, cols], ACT.Copy, scale=neg_dz[:])
            add_turned(cols, dz_xp, last=(cols == TWO_TERMS))
        xdz = tile("xdz", 1)
        nc.scalar.activation(xdz[:], s2[:], ACT.Identity, scale=neg_inv_z[:], bias=cross[:])
        xdz_p = tile("xdz_p", V)
        nc.gpsimd.tensor_scalar(xdz_p[:, ON_GPSIMD], p[:, ON_GPSIMD], xdz[:], 0.0, ALU.mult, ALU.add)
        dense_sb = tile("dense_sb", TWO_TERMS.stop)
        nc.gpsimd.tensor_tensor(dense_sb[:, ON_GPSIMD], xdz_p[:, ON_GPSIMD], base_dz_xp[:], ALU.add)
        turn_back(TWO_TERMS)
        for cols in THREE_TERMS:
            nc.scalar.activation(xdz_p[:, cols], p[:, cols], ACT.Copy, scale=xdz[:])
            add_turned(cols, xdz_p, last=True)
        for cols in THREE_TERMS:
            turn_back(cols)
        nc.vector.scalar_tensor_tensor(
            dense_sb[:, TWO_TERMS], p[:, TWO_TERMS], xdz[:], dense[TWO_TERMS.start][:, 0:HALF], ALU.mult, ALU.add
        )

        result = tile("result", V)

        def finish(engine, cols, dense_part, staged):
            engine.tensor_tensor(staged, dense_part, xs1[:, cols], ALU.add)
            nc.sync.dma_start(out=out[:, cols], in_=staged)

        for cols in (halves[0], TWO_TERMS):
            finish(nc.vector, cols, dense_sb[:, cols], result[:, cols])
        for cols in THREE_TERMS[:2]:
            finish(nc.vector, cols, dense[cols.start][:, 0 : cols.stop - cols.start], result[:, cols])
        spent = THREE_TERMS[1].start
        finish(nc.gpsimd, halves[1], dense_sb[:, halves[1]], turned[:, spent : spent + HALF])
        first = THREE_TERMS[2].start
        for cols in (slice(first, V - LAST_STORE), slice(V - LAST_STORE, V)):
            finish(nc.vector, cols, dense[first][:, cols.start - first : cols.stop - first], result[:, cols])
